import numpy as np
import ml_dtypes


def mxq(x, axis, fmt="e4m3"):
    dtype, down = {"e4m3": (ml_dtypes.float8_e4m3fn, 7), "e5m2": (ml_dtypes.float8_e5m2, 14)}[fmt]
    v = np.moveaxis(np.asarray(x, np.float32).astype(ml_dtypes.bfloat16).astype(np.float64), axis, -1)
    blocks = v.reshape(v.shape[:-1] + (-1, 32))
    amax = np.abs(blocks).max(-1, keepdims=True)
    byte = np.maximum(np.where(amax > 0, np.frexp(amax)[1] - 1 + 127, 0) - down, 1)
    scale = np.exp2(byte - 127.0)
    codes = (blocks / scale).astype(np.float32).astype(dtype).astype(np.float64)
    return np.moveaxis((codes * scale).reshape(v.shape), -1, axis)


WIDE = False


def mx_kscale(k):
    if not WIDE:
        return np.ones(k)
    levels = np.array([10, -10, 5, -5, 0])
    if k % 512:
        return np.exp2(np.random.permutation(np.resize(levels, k // 32))).repeat(32)
    a = np.empty((k // 512, 16))
    for p in range(k // 512):
        a[p, :8] = np.random.permutation(np.resize(levels, 8))
        for g in range(8):
            far = levels[np.abs(levels - a[p, g]) >= 10]
            a[p, g + 8] = far[np.random.randint(len(far))]
    return np.exp2(a.ravel()).repeat(32)


def f64(x):
    return np.asarray(x).astype(np.float64)


def striped(idx):
    return np.tile(idx.reshape(-1, 16).T, (8, 1)).astype(np.uint16)


def unstriped(offs):
    return offs[:16].T.reshape(-1).astype(np.int64)


E2M1 = np.array([0.0, 0.5, 1.0, 1.5, 2.0, 3.0, 4.0, 6.0, -0.0, -0.5, -1.0, -1.5, -2.0, -3.0, -4.0, -6.0])


def pack_weight(w, fmt):
    k, n = w.shape
    w = f64(np.asarray(w, np.float32).astype(ml_dtypes.bfloat16)).reshape(k // 32, 32, n)
    amax = np.abs(w).max(1)
    if fmt == "e4m3":
        byte = np.frexp(amax)[1] - 1 + 127 - 7
    else:
        mant, ex = np.frexp(amax / 6.0)
        byte = np.where(mant > 0.5, ex, ex - 1) + 127
    byte = np.clip(np.where(amax > 0, byte, 1), 1, 254)
    scaled = (w * np.exp2(127.0 - byte)[:, None, :]).reshape(k, n).astype(np.float32)
    by_word = np.ascontiguousarray(scaled.reshape(k // 512, 128, 4, n).transpose(0, 1, 3, 2))
    if fmt == "e4m3":
        words = by_word.astype(ml_dtypes.float8_e4m3fn).view(np.uint8)
    else:
        c = by_word.astype(ml_dtypes.float4_e2m1fn).view(np.uint8) & 0xF
        words = (c[..., 0::2] | (c[..., 1::2] << 4)).reshape(k // 512, 128, 2 * n)
    return np.ascontiguousarray(words), np.ascontiguousarray(byte.astype(np.uint8).reshape(k // 512, 16, n))


def unpack_weight(words, scales, fmt):
    g, _, n = scales.shape
    words = np.ascontiguousarray(words).reshape(g, 128, n, -1)
    if fmt == "e4m3":
        vals = words.view(ml_dtypes.float8_e4m3fn).astype(np.float64)
    else:
        nib = np.empty((g, 128, n, 4), np.uint8)
        nib[..., 0::2] = words & 0xF
        nib[..., 1::2] = words >> 4
        vals = E2M1[nib]
    vals = vals * np.repeat(np.exp2(scales.astype(np.float64) - 127.0), 8, axis=1)[..., None]
    return vals.transpose(0, 1, 3, 2).reshape(g * 512, n)


def gelu(v):
    return 0.5 * v * (1.0 + np.tanh(np.sqrt(2.0 / np.pi) * (v + 0.044715 * v**3)))


K, H, N, T, S = 1024, 1024, 512, 2048, 512

def setup_inputs():
    n = np.random.standard_normal
    s = mx_kscale(K)[:, None]
    u = mx_kscale(H)[:, None]
    tab_words, tab_scales = pack_weight(n((K, T)) * s, "e4m3")
    offs = striped(np.random.permutation(T)[:S])
    offs2 = striped(np.random.permutation(T)[:S])
    offs3 = striped(np.random.permutation(T)[:S])
    w1 = (n((K, H)) / np.sqrt(K) / s * u.T).astype(np.float32)
    w2_words, w2_scales = pack_weight(n((K, H)) / np.sqrt(K) / s, "e2m1")
    w3 = (n((K, H)) / np.sqrt(K) / s * u.T).astype(np.float32)
    w4_words, w4_scales = pack_weight(n((H, N)) / np.sqrt(H) / u, "e4m3")
    gain = np.exp(0.3 * n(N)).astype(np.float32)
    res = n((N, S)).astype(np.float32)
    return {"tab_words": tab_words, "tab_scales": tab_scales, "offs": offs, "offs2": offs2, "offs3": offs3,
            "w1": w1, "w2_words": w2_words, "w2_scales": w2_scales, "w3": w3,
            "w4_words": w4_words, "w4_scales": w4_scales, "gain": gain, "res": res}

def reference(tab_words, tab_scales, offs, offs2, offs3, w1, w2_words, w2_scales, w3, w4_words, w4_scales, gain, res):
    TW = unpack_weight(tab_words, tab_scales, "e4m3")
    v = TW[:, unstriped(offs)]
    v2 = TW[:, unstriped(offs2)]
    v3 = TW[:, unstriped(offs3)]
    w1q = mxq(f64(w1), 0, "e4m3")
    w2 = unpack_weight(w2_words, w2_scales, "e2m1")
    w3q = mxq(f64(w3), 0, "e4m3")
    w4 = unpack_weight(w4_words, w4_scales, "e4m3")
    upper = w1q.T @ v
    traffic = w2.T @ v2
    lower = w3q.T @ v3
    h = np.abs(upper - lower) * traffic + lower
    hq = mxq(h, 0, "e4m3")
    y = w4.T @ hq
    return f64(gain)[:, None] * y + f64(res)

@@ -1,0 +1,293 @@
+from contextlib import ExitStack
+
+import concourse.mybir as mybir
+from concourse.masks import make_identity
+
+K, H, N, T, S = 1024, 1024, 512, 2048, 512
+FLOPS = 2 * (3 * K * H * S + H * N * S)
+
+F32 = mybir.dt.float32
+BF16 = mybir.dt.bfloat16
+I32 = mybir.dt.int32
+U32 = mybir.dt.uint32
+U16 = mybir.dt.uint16
+U8 = mybir.dt.uint8
+FP8X4 = mybir.dt.float8_e4m3fn_x4
+FP4X4 = mybir.dt.float4_e2m1fn_x4
+ALU = mybir.AluOpType
+ACT = mybir.ActivationFunctionType
+
+P = 128
+PACK = 4
+K_PASS = P * PACK
+BLK = 256
+PASSES = 2
+
+
+def tile_list_rule_shadowing_conflicts_kernel(
+    tc, tab_words, tab_scales, offs, offs2, offs3, w1, w2_words, w2_scales, w3, w4_words, w4_scales, gain, res, out
+):
+    nc = tc.nc
+    with ExitStack() as ctx:
+        keep = ctx.enter_context(tc.tile_pool(name="keep", bufs=1))
+        ring = ctx.enter_context(tc.tile_pool(name="ring", bufs=3))
+        psum = ctx.enter_context(tc.psum_pool(name="psum", bufs=2))
+
+        lists = {}
+
+        def load_list(name):
+            lists[name] = keep.tile([P, S // 16], U16, name=f"list_{name}")
+            nc.sync.dma_start(lists[name][:], {"lower": offs3, "upper": offs, "traffic": offs2}[name])
+
+        tab_sc = keep.tile([P, T], U8, align_bytes=64)
+        tab_sc1 = keep.tile([P, T], U8, align_bytes=64)
+        w2_sc = keep.tile([P, PASSES, H], U8, align_bytes=64)
+        w4_sc = keep.tile([P, N], U8, align_bytes=64)
+        nc.vector.memset(tab_sc[:].bitcast(I32), 0)
+        nc.vector.memset(tab_sc1[:].bitcast(I32), 0)
+        nc.vector.memset(w2_sc[:].rearrange("p a c -> p (a c)").bitcast(I32), 0)
+        nc.vector.memset(w4_sc[:].bitcast(I32), 0)
+
+        def load_tab_scales():
+            for q in range(4):
+                nc.sync.dma_start(
+                    tab_sc[32 * q : 32 * q + 8, :].bitcast(I32), tab_scales[:, 4 * q : 4 * q + 4, :].bitcast(I32)
+                )
+
+        def load_traffic_scales(eng):
+            for q in range(4):
+                eng.dma_start(
+                    tab_sc1[32 * q : 32 * q + 4, :].bitcast(I32), tab_scales[1, 4 * q : 4 * q + 4, :].bitcast(I32)
+                )
+
+        def load_w2_scales(eng):
+            for q in range(4):
+                eng.dma_start(
+                    w2_sc[32 * q : 32 * q + 4, :, :].bitcast(I32),
+                    w2_scales[:, 4 * q : 4 * q + 4, :].rearrange("a r c -> r a c").bitcast(I32),
+                )
+
+        ident = keep.tile([P, P], F32)
+        make_identity(nc, ident[:])
+
+        tab = [keep.tile([P, T], I32, name=f"tab{a}", align_bytes=64) for a in range(PASSES)]
+        w2_t = keep.tile([P, PASSES, 2 * H], U8, align_bytes=64)
+        w4_t = keep.tile([P, PASSES, N], I32, align_bytes=64)
+        res_t = keep.tile([P, 4, S], F32)
+        gain_t = keep.tile([P, 4], F32)
+        raw = {}
+
+        def load_tab(a, pieces):
+            src = tab_words[a].rearrange("p t i -> p (t i)").bitcast(I32)
+            for i in range(pieces):
+                cols = slice(i * T // pieces, (i + 1) * T // pieces)
+                nc.sync.dma_start(tab[a][:, cols], src[:, cols])
+
+        def load_gain():
+            with nc.allow_non_contiguous_dma(reason="one gain a partition"):
+                nc.sync.dma_start(gain_t[:], gain.rearrange("(t p) -> p t", p=P))
+
+        def load_w4_scales(eng):
+            for q in range(4):
+                eng.dma_start(
+                    w4_sc[32 * q : 32 * q + 8, :].bitcast(I32), w4_scales[:, 4 * q : 4 * q + 4, :].bitcast(I32)
+                )
+
+        def load_w(name, a, blk, nblk):
+            src = {"lower": w3, "upper": w1}[name]
+            t = keep.tile([P, PACK, nblk * BLK], F32, name=f"raw_{name}{a}_{blk}")
+            rows = src[a * K_PASS : (a + 1) * K_PASS, blk * BLK : (blk + nblk) * BLK]
+            nc.sync.dma_start(t[:], rows.rearrange("(p j) c -> p j c", j=PACK))
+            for i in range(nblk):
+                raw[name, a, blk + i] = t[:, :, i * BLK : (i + 1) * BLK]
+
+        def load_w4():
+            nc.sync.dma_start(w4_t[:], w4_words.rearrange("a p c i -> p a (c i)").bitcast(I32))
+
+        def load_res():
+            nc.sync.dma_start(res_t[:], res.rearrange("(t p) j -> p t j", p=P))
+
+        def load_w2():
+            nc.sync.dma_start(w2_t[:].bitcast(I32), w2_words.rearrange("a p c -> p a c").bitcast(I32))
+
+        load_list("lower")
+        load_list("upper")
+        load_list("traffic")
+        load_tab(0, 2)
+        load_tab_scales()
+        load_w("lower", 0, 0, 1)
+        load_w("lower", 1, 0, 1)
+        load_w("upper", 0, 0, 1)
+        load_w("upper", 1, 0, 1)
+        load_traffic_scales(nc.sync)
+        load_w("lower", 0, 1, 1)
+        load_w("lower", 1, 1, 1)
+        load_tab(1, 1)
+        load_w2()
+        load_w2_scales(nc.sync)
+        load_w("upper", 0, 1, 1)
+        load_w("upper", 1, 1, 1)
+        load_w("lower", 0, 2, 2)
+        load_w4_scales(nc.sync)
+        load_w("lower", 1, 2, 2)
+        load_w("upper", 0, 2, 1)
+        load_w("upper", 1, 2, 1)
+        load_w("upper", 0, 3, 1)
+        load_w("upper", 1, 3, 1)
+        load_gain()
+        load_w4()
+        load_res()
+
+        words, scales = {}, {}
+
+        def gather_words(name, a):
+            words[name, a] = keep.tile([P, S], U32, name=f"words_{name}{a}", align_bytes=64)
+            nc.vector.tensor_copy(words[name, a][:], tab[a][:].bitcast(U32).indirect(lists[name][:]))
+
+        def gather_scales(name):
+            g = keep.tile([P, S], U8, name=f"scales_{name}", align_bytes=64)
+            nc.vector.tensor_copy(g[:], tab_sc[:].indirect(lists[name][:]))
+            scales[name, 0] = g[:]
+            scales[name, 1] = g[4:P, :]
+
+        gather_words("lower", 0)
+        gather_words("upper", 0)
+        gather_scales("lower")
+        gather_scales("upper")
+        gather_words("lower", 1)
+        gather_words("upper", 1)
+
+        def gather_traffic():
+            gather_scales("traffic")
+            gather_words("traffic", 0)
+            gather_words("traffic", 1)
+            traffic_sc1 = keep.tile([P, S], U8, align_bytes=64)
+            nc.vector.tensor_copy(traffic_sc1[:], tab_sc1[:].indirect(lists["traffic"][:]))
+            scales["traffic", 1] = traffic_sc1[:]
+
+        wq, wq_sc = {}, {}
+        banks = {"ly": 2, "u": 2, "t": 2, "h": 2}
+        h_tag = (("h",) * 4, ("h", "h", "ly", "ly"))
+        y_tag = ("u", "t", "u", "t")
+        on_vector = {("upper", 1, 1), ("lower", 1, 2), ("upper", 1, 2), ("upper", 1, 3)}
+        on_gpsimd = set()
+
+        def quantize_w(name, a, blk):
+            key = (name, a, blk)
+            grouped = ring.tile([P, BLK, PACK], BF16, name="grouped", align_bytes=64, bufs=8)
+            dst = grouped[:].rearrange("p (c i) t -> p c t i", i=4)
+            src = raw[key].rearrange("p t (c i) -> p c t i", i=4)
+            if key in on_vector:
+                nc.vector.tensor_copy(dst, src)
+            elif key in on_gpsimd:
+                nc.gpsimd.tensor_scalar(dst, src, 1.0, 0.0, ALU.mult, ALU.add)
+            else:
+                nc.scalar.activation(dst, src, ACT.Copy)
+            wq[key] = keep.tile([P, BLK], U32, name=f"wq_{name}{a}_{blk}", align_bytes=64)
+            wq_sc[key] = keep.tile([P, BLK], U8, name=f"wqsc_{name}{a}_{blk}", align_bytes=64)
+            nc.vector.quantize_mx(wq[key][:].bitcast(FP8X4), wq_sc[key][:], grouped[:].rearrange("p c t -> p (c t)"))
+
+        def first_product(name, blk, pair, tag):
+            bank = psum.tile([P, 2, BLK], F32, name=f"bank_{name}", tag=tag, bufs=banks[tag])
+            for i in range(2):
+                cols = slice((2 * pair + i) * P, (2 * pair + i + 1) * P)
+                for a in range(PASSES):
+                    if name == "traffic":
+                        rhs = w2_t[:, a, 2 * blk * BLK : 2 * (blk + 1) * BLK].bitcast(FP4X4)
+                        rhs_sc = w2_sc[:, a, blk * BLK : (blk + 1) * BLK]
+                    else:
+                        rhs = wq[name, a, blk][:].bitcast(FP8X4)
+                        rhs_sc = wq_sc[name, a, blk][:]
+                    nc.tensor.matmul_mx(
+                        bank[:, i, :],
+                        lhsT=words[name, a][:, cols].bitcast(FP8X4),
+                        lhsT_scale=scales[name, a][:, cols],
+                        rhs=rhs,
+                        rhs_scale=rhs_sc,
+                        start=(a == 0),
+                        stop=(a == PASSES - 1),
+                    )
+            return bank[:].rearrange("j i (p t) -> j i t p", t=PACK)
+
+        lower, weighted, hq, hq_sc = {}, {}, {}, {}
+        for b in range(PASSES):
+            for pair in range(2):
+                lower[b, pair] = keep.tile([P, 2, PACK, P], F32, name=f"lower{b}{pair}")
+                weighted[b, pair] = keep.tile([P, 2, PACK, P], F32, name=f"weighted{b}{pair}")
+
+        def copy_lower(blk, pair):
+            b, half = divmod(blk, 2)
+            nc.scalar.activation(
+                lower[b, pair][:, :, :, 64 * half : 64 * (half + 1)], first_product("lower", blk, pair, "ly"), ACT.Copy
+            )
+
+        def combine(blk, pair):
+            b, half = divmod(blk, 2)
+            part = slice(64 * half, 64 * (half + 1))
+            diff = ring.tile([P, 2, PACK, 64], F32, name="diff")
+            nc.vector.tensor_tensor(
+                diff[:], first_product("upper", blk, pair, "u"), lower[b, pair][:, :, :, part], ALU.subtract
+            )
+            dist = ring.tile([P, 2, PACK, 64], F32, name="dist")
+            nc.scalar.activation(dist[:], diff[:], ACT.Abs)
+            nc.vector.tensor_tensor(
+                weighted[b, pair][:, :, :, part], first_product("traffic", blk, pair, "t"), dist[:], ALU.mult
+            )
+
+        def make_h(b, jc):
+            pair, i = divmod(jc, 2)
+            bank = psum.tile([P, PACK, P], F32, name="bank_h", tag=h_tag[b][jc], bufs=banks[h_tag[b][jc]])
+            terms = (lower[b, pair], weighted[b, pair])
+            for n, term in enumerate(terms):
+                for t in range(PACK):
+                    nc.tensor.matmul(
+                        bank[:, t, :],
+                        lhsT=term[:, i, t, :],
+                        rhs=ident[:],
+                        is_transpose=True,
+                        start=(n == 0 and t == 0),
+                        stop=(n == 1 and t == PACK - 1),
+                    )
+            h = ring.tile([P, P, PACK], BF16, name="h", align_bytes=64)
+            nc.scalar.activation(h[:], bank[:].rearrange("p t j -> p j t"), ACT.Copy)
+            hq[b, jc] = keep.tile([P, P], U32, name=f"hq{b}{jc}", align_bytes=64)
+            hq_sc[b, jc] = keep.tile([P, P], U8, name=f"hqsc{b}{jc}", align_bytes=64)
+            nc.vector.quantize_mx(hq[b, jc][:].bitcast(FP8X4), hq_sc[b, jc][:], h[:].rearrange("p j t -> p (j t)"))
+
+        def finish(jc):
+            cols = slice(jc * P, (jc + 1) * P)
+            bank = psum.tile([P, 4, P], F32, name="bank_y", tag=y_tag[jc], bufs=banks[y_tag[jc]])
+            for n, b in enumerate((1, 0)):
+                for nt in range(4):
+                    nc.tensor.matmul_mx(
+                        bank[:, nt, :],
+                        lhsT=w4_t[:, b, nt * P : (nt + 1) * P].bitcast(FP8X4),
+                        lhsT_scale=w4_sc[4 * b : P, nt * P : (nt + 1) * P],
+                        rhs=hq[b, jc][:].bitcast(FP8X4),
+                        rhs_scale=hq_sc[b, jc][:],
+                        start=(n == 0 and nt == 0),
+                        stop=(n == 1 and nt == 3),
+                    )
+            result = keep.tile([P, 4, P], F32, name=f"result{jc}")
+            for nt in range(4):
+                nc.vector.scalar_tensor_tensor(
+                    result[:, nt, :], bank[:, nt, :], gain_t[:, nt : nt + 1], res_t[:, nt, cols], ALU.mult, ALU.add
+                )
+            nc.sync.dma_start(out.rearrange("(t p) j -> p t j", p=P)[:, :, cols], result[:])
+
+        for blk in range(4):
+            for a in range(PASSES):
+                quantize_w("lower", a, blk)
+            for pair in range(2):
+                copy_lower(blk, pair)
+            for a in range(PASSES):
+                quantize_w("upper", a, blk)
+            if blk == 0:
+                gather_traffic()
+            for pair in range(2):
+                combine(blk, pair)
+            if blk % 2 == 1:
+                for jc in range(4):
+                    make_h(blk // 2, jc)
+        for jc in range(4):
+            finish(jc)

@@ -40,24 +40,18 @@ def tile_list_rule_shadowing_conflicts_kernel(
             nc.sync.dma_start(lists[name][:], {"lower": offs3, "upper": offs, "traffic": offs2}[name])
 
         tab_sc = keep.tile([P, T], U8, align_bytes=64)
-        tab_sc1 = keep.tile([P, T], U8, align_bytes=64)
         w2_sc = keep.tile([P, PASSES, H], U8, align_bytes=64)
         w4_sc = keep.tile([P, N], U8, align_bytes=64)
-        nc.vector.memset(tab_sc[:].bitcast(I32), 0)
-        nc.vector.memset(tab_sc1[:].bitcast(I32), 0)
+        traffic_sc1 = keep.tile([P, S], U8, align_bytes=64)
         nc.vector.memset(w2_sc[:].rearrange("p a c -> p (a c)").bitcast(I32), 0)
+        nc.vector.memset(tab_sc[:].bitcast(I32), 0)
         nc.vector.memset(w4_sc[:].bitcast(I32), 0)
+        nc.vector.memset(traffic_sc1[:].bitcast(I32), 0)
 
         def load_tab_scales():
             for q in range(4):
                 nc.sync.dma_start(
                     tab_sc[32 * q : 32 * q + 8, :].bitcast(I32), tab_scales[:, 4 * q : 4 * q + 4, :].bitcast(I32)
-                )
-
-        def load_traffic_scales(eng):
-            for q in range(4):
-                eng.dma_start(
-                    tab_sc1[32 * q : 32 * q + 4, :].bitcast(I32), tab_scales[1, 4 * q : 4 * q + 4, :].bitcast(I32)
                 )
 
         def load_w2_scales(eng):
@@ -114,21 +108,20 @@ def tile_list_rule_shadowing_conflicts_kernel(
         load_list("upper")
         load_list("traffic")
         load_tab(0, 2)
-        load_tab_scales()
+        load_tab(1, 2)
+        load_w2_scales(nc.gpsimd)
+        load_w4_scales(nc.gpsimd)
         load_w("lower", 0, 0, 1)
         load_w("lower", 1, 0, 1)
         load_w("upper", 0, 0, 1)
         load_w("upper", 1, 0, 1)
-        load_traffic_scales(nc.sync)
+        load_tab_scales()
         load_w("lower", 0, 1, 1)
         load_w("lower", 1, 1, 1)
-        load_tab(1, 1)
-        load_w2()
-        load_w2_scales(nc.sync)
         load_w("upper", 0, 1, 1)
         load_w("upper", 1, 1, 1)
+        load_w2()
         load_w("lower", 0, 2, 2)
-        load_w4_scales(nc.sync)
         load_w("lower", 1, 2, 2)
         load_w("upper", 0, 2, 1)
         load_w("upper", 1, 2, 1)
@@ -150,26 +143,21 @@ def tile_list_rule_shadowing_conflicts_kernel(
             scales[name, 0] = g[:]
             scales[name, 1] = g[4:P, :]
 
-        gather_words("lower", 0)
-        gather_words("upper", 0)
-        gather_scales("lower")
-        gather_scales("upper")
-        gather_words("lower", 1)
-        gather_words("upper", 1)
-
-        def gather_traffic():
-            gather_scales("traffic")
-            gather_words("traffic", 0)
-            gather_words("traffic", 1)
-            traffic_sc1 = keep.tile([P, S], U8, align_bytes=64)
-            nc.vector.tensor_copy(traffic_sc1[:], tab_sc1[:].indirect(lists["traffic"][:]))
+        def shift_traffic_scales(eng):
+            eng.dma_start(traffic_sc1[0:100, :].bitcast(I32), scales["traffic", 0][4:104, :].bitcast(I32))
             scales["traffic", 1] = traffic_sc1[:]
 
+        for a in range(PASSES):
+            for name in ("lower", "upper", "traffic"):
+                gather_words(name, a)
+        gather_scales("traffic")
+        shift_traffic_scales(nc.gpsimd)
+        gather_scales("lower")
+        gather_scales("upper")
+
         wq, wq_sc = {}, {}
-        banks = {"ly": 2, "u": 2, "t": 2, "h": 2}
-        h_tag = (("h",) * 4, ("h", "h", "ly", "ly"))
-        y_tag = ("u", "t", "u", "t")
-        on_vector = {("upper", 1, 1), ("lower", 1, 2), ("upper", 1, 2), ("upper", 1, 3)}
+        banks = {"l": 2, "u": 2, "t": 2, "h": 2}
+        on_vector = {("lower", 1, 1), ("upper", 1, 1), ("lower", 1, 2), ("upper", 1, 2), ("upper", 1, 3)}
         on_gpsimd = set()
 
         def quantize_w(name, a, blk):
@@ -187,10 +175,10 @@ def tile_list_rule_shadowing_conflicts_kernel(
             wq_sc[key] = keep.tile([P, BLK], U8, name=f"wqsc_{name}{a}_{blk}", align_bytes=64)
             nc.vector.quantize_mx(wq[key][:].bitcast(FP8X4), wq_sc[key][:], grouped[:].rearrange("p c t -> p (c t)"))
 
-        def first_product(name, blk, pair, tag):
-            bank = psum.tile([P, 2, BLK], F32, name=f"bank_{name}", tag=tag, bufs=banks[tag])
-            for i in range(2):
-                cols = slice((2 * pair + i) * P, (2 * pair + i + 1) * P)
+        def first_product(name, blk, jc0, count, tag):
+            bank = psum.tile([P, count, BLK], F32, name=f"bank_{name}", tag=tag, bufs=banks[tag])
+            for i in range(count):
+                cols = slice((jc0 + i) * P, (jc0 + i + 1) * P)
                 for a in range(PASSES):
                     if name == "traffic":
                         rhs = w2_t[:, a, 2 * blk * BLK : 2 * (blk + 1) * BLK].bitcast(FP4X4)
@@ -207,87 +195,112 @@ def tile_list_rule_shadowing_conflicts_kernel(
                         start=(a == 0),
                         stop=(a == PASSES - 1),
                     )
-            return bank[:].rearrange("j i (p t) -> j i t p", t=PACK)
+            return bank[:]
 
-        lower, weighted, hq, hq_sc = {}, {}, {}, {}
+        lower, h, hq, hq_sc = {}, {}, {}, {}
+        add_on_gpsimd = set()
         for b in range(PASSES):
             for pair in range(2):
-                lower[b, pair] = keep.tile([P, 2, PACK, P], F32, name=f"lower{b}{pair}")
-                weighted[b, pair] = keep.tile([P, 2, PACK, P], F32, name=f"weighted{b}{pair}")
+                h[b, pair] = keep.tile([P, 2, K_PASS], BF16, name=f"h{b}{pair}")
 
         def copy_lower(blk, pair):
-            b, half = divmod(blk, 2)
-            nc.scalar.activation(
-                lower[b, pair][:, :, :, 64 * half : 64 * (half + 1)], first_product("lower", blk, pair, "ly"), ACT.Copy
-            )
+            lower[blk, pair] = ring.tile([P, 2, BLK], F32, name="lower", bufs=8)
+            nc.scalar.activation(lower[blk, pair][:], first_product("lower", blk, 2 * pair, 2, "l"), ACT.Copy)
 
-        def combine(blk, pair):
+        def combine(blk, jc0, count):
             b, half = divmod(blk, 2)
-            part = slice(64 * half, 64 * (half + 1))
-            diff = ring.tile([P, 2, PACK, 64], F32, name="diff")
-            nc.vector.tensor_tensor(
-                diff[:], first_product("upper", blk, pair, "u"), lower[b, pair][:, :, :, part], ALU.subtract
-            )
-            dist = ring.tile([P, 2, PACK, 64], F32, name="dist")
+            pair, within = divmod(jc0, 2)
+            low = lower[blk, pair][:, within : within + count, :]
+            diff = ring.tile([P, count, BLK], F32, name="diff")
+            nc.vector.tensor_tensor(diff[:], first_product("upper", blk, jc0, count, "u"), low, ALU.subtract)
+            dist = ring.tile([P, count, BLK], F32, name="dist", bufs=4)
             nc.scalar.activation(dist[:], diff[:], ACT.Abs)
-            nc.vector.tensor_tensor(
-                weighted[b, pair][:, :, :, part], first_product("traffic", blk, pair, "t"), dist[:], ALU.mult
+            weighted = ring.tile([P, count, BLK], F32, name="weighted")
+            nc.vector.tensor_tensor(weighted[:], first_product("traffic", blk, jc0, count, "t"), dist[:], ALU.mult)
+            adder = nc.gpsimd if (blk, pair) in add_on_gpsimd else nc.vector
+            adder.tensor_tensor(
+                h[b, pair][:, within : within + count, half * BLK : (half + 1) * BLK], weighted[:], low, ALU.add
             )
 
-        def make_h(b, jc):
-            pair, i = divmod(jc, 2)
-            bank = psum.tile([P, PACK, P], F32, name="bank_h", tag=h_tag[b][jc], bufs=banks[h_tag[b][jc]])
-            terms = (lower[b, pair], weighted[b, pair])
-            for n, term in enumerate(terms):
-                for t in range(PACK):
-                    nc.tensor.matmul(
-                        bank[:, t, :],
-                        lhsT=term[:, i, t, :],
-                        rhs=ident[:],
-                        is_transpose=True,
-                        start=(n == 0 and t == 0),
-                        stop=(n == 1 and t == PACK - 1),
-                    )
-            h = ring.tile([P, P, PACK], BF16, name="h", align_bytes=64)
-            nc.scalar.activation(h[:], bank[:].rearrange("p t j -> p j t"), ACT.Copy)
-            hq[b, jc] = keep.tile([P, P], U32, name=f"hq{b}{jc}", align_bytes=64)
-            hq_sc[b, jc] = keep.tile([P, P], U8, name=f"hqsc{b}{jc}", align_bytes=64)
-            nc.vector.quantize_mx(hq[b, jc][:].bitcast(FP8X4), hq_sc[b, jc][:], h[:].rearrange("p j t -> p (j t)"))
+        def make_h(b, jc0, count, tag):
+            bank = psum.tile([P, count, 2, P], F32, name="bank_h", tag=tag, bufs=banks[tag])
+            for i in range(count):
+                pair, within = divmod(jc0 + i, 2)
+                pairs = h[b, pair][:, within, :].bitcast(F32)
+                for u in range(2):
+                    nc.tensor.transpose(bank[:, i, u, :], pairs[:, u::2], ident[:])
+            h_t = ring.tile([P, count, P, 2], F32, name="h_t", align_bytes=64)
+            nc.scalar.copy(h_t[:], bank[:].rearrange("p i u j -> p i j u"))
+            codes = keep.tile([P, count * P], U32, name=f"hq{b}{jc0}", align_bytes=64)
+            plane = keep.tile([P, count * P], U8, name=f"hqsc{b}{jc0}", align_bytes=64)
+            nc.vector.quantize_mx(
+                codes[:].bitcast(FP8X4), plane[:], h_t[:].rearrange("p i j u -> p (i j u)").bitcast(BF16)
+            )
+            for i in range(count):
+                hq[b, jc0 + i] = (codes, plane, i * P)
 
-        def finish(jc):
-            cols = slice(jc * P, (jc + 1) * P)
-            bank = psum.tile([P, 4, P], F32, name="bank_y", tag=y_tag[jc], bufs=banks[y_tag[jc]])
-            for n, b in enumerate((1, 0)):
-                for nt in range(4):
-                    nc.tensor.matmul_mx(
-                        bank[:, nt, :],
-                        lhsT=w4_t[:, b, nt * P : (nt + 1) * P].bitcast(FP8X4),
-                        lhsT_scale=w4_sc[4 * b : P, nt * P : (nt + 1) * P],
-                        rhs=hq[b, jc][:].bitcast(FP8X4),
-                        rhs_scale=hq_sc[b, jc][:],
-                        start=(n == 0 and nt == 0),
-                        stop=(n == 1 and nt == 3),
+        def finish(jc0, count, tags):
+            width = count * P
+            cols = slice(jc0 * P, jc0 * P + width)
+            per_bank = 4 // count
+            for g, tag in enumerate(tags):
+                bank = psum.tile([P, per_bank, width], F32, name="bank_y", tag=tag, bufs=banks[tag])
+                for n, b in enumerate((1, 0)):
+                    codes, plane, c0 = hq[b, jc0]
+                    for i in range(per_bank):
+                        nt = g * per_bank + i
+                        nc.tensor.matmul_mx(
+                            bank[:, i, :],
+                            lhsT=w4_t[:, b, nt * P : (nt + 1) * P].bitcast(FP8X4),
+                            lhsT_scale=w4_sc[4 * b : P, nt * P : (nt + 1) * P],
+                            rhs=codes[:, c0 : c0 + width].bitcast(FP8X4),
+                            rhs_scale=plane[:, c0 : c0 + width],
+                            start=(n == 0 and i == 0),
+                            stop=(n == 1 and i == per_bank - 1),
+                        )
+                result = keep.tile([P, per_bank, width], F32, name=f"result{jc0}{g}")
+                for i in range(per_bank):
+                    nt = g * per_bank + i
+                    nc.vector.scalar_tensor_tensor(
+                        result[:, i, :], bank[:, i, :], gain_t[:, nt : nt + 1], res_t[:, nt, cols], ALU.mult, ALU.add
                     )
-            result = keep.tile([P, 4, P], F32, name=f"result{jc}")
-            for nt in range(4):
-                nc.vector.scalar_tensor_tensor(
-                    result[:, nt, :], bank[:, nt, :], gain_t[:, nt : nt + 1], res_t[:, nt, cols], ALU.mult, ALU.add
-                )
-            nc.sync.dma_start(out.rearrange("(t p) j -> p t j", p=P)[:, :, cols], result[:])
+                rows = out.rearrange("(t p) j -> p t j", p=P)[:, g * per_bank : (g + 1) * per_bank, cols]
+                nc.sync.dma_start(rows, result[:])
 
-        for blk in range(4):
-            for a in range(PASSES):
-                quantize_w("lower", a, blk)
-            for pair in range(2):
-                copy_lower(blk, pair)
-            for a in range(PASSES):
-                quantize_w("upper", a, blk)
-            if blk == 0:
-                gather_traffic()
-            for pair in range(2):
-                combine(blk, pair)
-            if blk % 2 == 1:
-                for jc in range(4):
-                    make_h(blk // 2, jc)
+        for a in range(PASSES):
+            quantize_w("lower", a, 0)
+        for a in range(PASSES):
+            quantize_w("upper", a, 0)
+        for a in range(PASSES):
+            quantize_w("lower", a, 1)
+        for a in range(PASSES):
+            quantize_w("upper", a, 1)
+        for pair in range(2):
+            copy_lower(0, pair)
+        for pair in range(2):
+            copy_lower(1, pair)
+        for a in range(PASSES):
+            quantize_w("lower", a, 2)
+        for a in range(PASSES):
+            quantize_w("lower", a, 3)
+        combine(0, 0, 2)
+        combine(0, 2, 2)
+        combine(1, 0, 2)
+        combine(1, 2, 2)
+        for pair in range(2):
+            copy_lower(2, pair)
+        for pair in range(2):
+            copy_lower(3, pair)
+        for a in range(PASSES):
+            quantize_w("upper", a, 2)
+        for a in range(PASSES):
+            quantize_w("upper", a, 3)
+        make_h(0, 0, 2, "h")
+        make_h(0, 2, 2, "h")
+        combine(2, 0, 2)
+        combine(2, 2, 2)
         for jc in range(4):
-            finish(jc)
+            combine(3, jc, 1)
+        for jc in range(4):
+            make_h(1, jc, 1, "h")
+            finish(jc, 1, ("l",))

@@ -22,6 +22,7 @@ PACK = 4
 K_PASS = P * PACK
 BLK = 256
 PASSES = 2
+LAST = 3
 
 
 def tile_list_rule_shadowing_conflicts_kernel(
@@ -108,28 +109,12 @@ def tile_list_rule_shadowing_conflicts_kernel(
         load_list("upper")
         load_list("traffic")
         load_tab(0, 2)
-        load_tab(1, 2)
+        load_tab_scales()
         load_w2_scales(nc.gpsimd)
         load_w4_scales(nc.gpsimd)
         load_w("lower", 0, 0, 1)
         load_w("lower", 1, 0, 1)
         load_w("upper", 0, 0, 1)
-        load_w("upper", 1, 0, 1)
-        load_tab_scales()
-        load_w("lower", 0, 1, 1)
-        load_w("lower", 1, 1, 1)
-        load_w("upper", 0, 1, 1)
-        load_w("upper", 1, 1, 1)
-        load_w2()
-        load_w("lower", 0, 2, 2)
-        load_w("lower", 1, 2, 2)
-        load_w("upper", 0, 2, 1)
-        load_w("upper", 1, 2, 1)
-        load_w("upper", 0, 3, 1)
-        load_w("upper", 1, 3, 1)
-        load_gain()
-        load_w4()
-        load_res()
 
         words, scales = {}, {}
 
@@ -147,54 +132,77 @@ def tile_list_rule_shadowing_conflicts_kernel(
             eng.dma_start(traffic_sc1[0:100, :].bitcast(I32), scales["traffic", 0][4:104, :].bitcast(I32))
             scales["traffic", 1] = traffic_sc1[:]
 
-        for a in range(PASSES):
-            for name in ("lower", "upper", "traffic"):
-                gather_words(name, a)
+        for name in ("lower", "upper", "traffic"):
+            gather_words(name, 0)
         gather_scales("traffic")
-        shift_traffic_scales(nc.gpsimd)
+        shift_traffic_scales(nc.sync)
+        load_w("upper", 1, 0, 1)
+        load_w("lower", 0, 1, 1)
+        load_w("lower", 1, 1, 1)
+        load_tab(1, 1)
+        load_w("upper", 0, 1, 1)
+        load_w2()
+        load_w("upper", 1, 1, 1)
+        load_w("lower", 0, 2, 1)
+        load_w("lower", 1, 2, 1)
+        load_w("upper", 0, 2, 1)
+        load_w("upper", 1, 2, 1)
+        load_w("lower", 0, 3, 1)
+        load_w("lower", 1, 3, 1)
+        load_w("upper", 0, 3, 1)
+        load_w("upper", 1, 3, 1)
+        load_gain()
+        load_w4()
+        load_res()
         gather_scales("lower")
         gather_scales("upper")
+        for name in ("lower", "upper", "traffic"):
+            gather_words(name, 1)
 
         wq, wq_sc = {}, {}
         banks = {"l": 2, "u": 2, "t": 2, "h": 2}
-        on_vector = {("lower", 1, 1), ("upper", 1, 1), ("lower", 1, 2), ("upper", 1, 2), ("upper", 1, 3)}
+        on_vector = {("upper", 1, 1), ("upper", 1, 2), ("upper", 1, 3)}
         on_gpsimd = set()
 
-        def quantize_w(name, a, blk):
-            key = (name, a, blk)
-            grouped = ring.tile([P, BLK, PACK], BF16, name="grouped", align_bytes=64, bufs=8)
-            dst = grouped[:].rearrange("p (c i) t -> p c t i", i=4)
-            src = raw[key].rearrange("p t (c i) -> p c t i", i=4)
-            if key in on_vector:
-                nc.vector.tensor_copy(dst, src)
-            elif key in on_gpsimd:
-                nc.gpsimd.tensor_scalar(dst, src, 1.0, 0.0, ALU.mult, ALU.add)
-            else:
-                nc.scalar.activation(dst, src, ACT.Copy)
-            wq[key] = keep.tile([P, BLK], U32, name=f"wq_{name}{a}_{blk}", align_bytes=64)
-            wq_sc[key] = keep.tile([P, BLK], U8, name=f"wqsc_{name}{a}_{blk}", align_bytes=64)
-            nc.vector.quantize_mx(wq[key][:].bitcast(FP8X4), wq_sc[key][:], grouped[:].rearrange("p c t -> p (c t)"))
+        def quantize_w(name, blk):
+            grouped = ring.tile([P, PASSES, BLK, PACK], BF16, name="grouped", align_bytes=64, bufs=5)
+            sign = -1.0 if (name, blk) == ("upper", LAST) else 1.0
+            for a in range(PASSES):
+                dst = grouped[:, a, :, :].rearrange("p (c i) t -> p c t i", i=4)
+                src = raw[name, a, blk].rearrange("p t (c i) -> p c t i", i=4)
+                if (name, a, blk) in on_vector and sign == 1.0:
+                    nc.vector.tensor_copy(dst, src)
+                elif (name, a, blk) in on_vector:
+                    nc.vector.tensor_scalar(dst, src, sign, None, ALU.mult)
+                else:
+                    nc.scalar.activation(dst, src, ACT.Copy, scale=sign)
+            codes = keep.tile([P, PASSES * BLK], U32, name=f"wq_{name}{blk}", align_bytes=64)
+            plane = keep.tile([P, PASSES * BLK], U8, name=f"wqsc_{name}{blk}", align_bytes=64)
+            nc.vector.quantize_mx(codes[:].bitcast(FP8X4), plane[:], grouped[:].rearrange("p a c t -> p (a c t)"))
+            for a in range(PASSES):
+                wq[name, a, blk] = codes[:, a * BLK : (a + 1) * BLK]
+                wq_sc[name, a, blk] = plane[:, a * BLK : (a + 1) * BLK]
 
-        def first_product(name, blk, jc0, count, tag):
-            bank = psum.tile([P, count, BLK], F32, name=f"bank_{name}", tag=tag, bufs=banks[tag])
-            for i in range(count):
+        def first_product(names, blk, jc0, count, tag):
+            bank = psum.tile([P, count, BLK], F32, name=f"bank_{names[-1]}", tag=tag, bufs=banks[tag])
+            steps = [(name, a, i) for name in names for i in range(count) for a in range(PASSES)]
+            for n, (name, a, i) in enumerate(steps):
                 cols = slice((jc0 + i) * P, (jc0 + i + 1) * P)
-                for a in range(PASSES):
-                    if name == "traffic":
-                        rhs = w2_t[:, a, 2 * blk * BLK : 2 * (blk + 1) * BLK].bitcast(FP4X4)
-                        rhs_sc = w2_sc[:, a, blk * BLK : (blk + 1) * BLK]
-                    else:
-                        rhs = wq[name, a, blk][:].bitcast(FP8X4)
-                        rhs_sc = wq_sc[name, a, blk][:]
-                    nc.tensor.matmul_mx(
-                        bank[:, i, :],
-                        lhsT=words[name, a][:, cols].bitcast(FP8X4),
-                        lhsT_scale=scales[name, a][:, cols],
-                        rhs=rhs,
-                        rhs_scale=rhs_sc,
-                        start=(a == 0),
-                        stop=(a == PASSES - 1),
-                    )
+                if name == "traffic":
+                    rhs = w2_t[:, a, 2 * blk * BLK : 2 * (blk + 1) * BLK].bitcast(FP4X4)
+                    rhs_sc = w2_sc[:, a, blk * BLK : (blk + 1) * BLK]
+                else:
+                    rhs = wq[name, a, blk].bitcast(FP8X4)
+                    rhs_sc = wq_sc[name, a, blk]
+                nc.tensor.matmul_mx(
+                    bank[:, i, :],
+                    lhsT=words[name, a][:, cols].bitcast(FP8X4),
+                    lhsT_scale=scales[name, a][:, cols],
+                    rhs=rhs,
+                    rhs_scale=rhs_sc,
+                    start=(n == 0),
+                    stop=(n == len(steps) - 1),
+                )
             return bank[:]
 
         lower, h, hq, hq_sc = {}, {}, {}, {}
@@ -204,22 +212,38 @@ def tile_list_rule_shadowing_conflicts_kernel(
                 h[b, pair] = keep.tile([P, 2, K_PASS], BF16, name=f"h{b}{pair}")
 
         def copy_lower(blk, pair):
-            lower[blk, pair] = ring.tile([P, 2, BLK], F32, name="lower", bufs=8)
-            nc.scalar.activation(lower[blk, pair][:], first_product("lower", blk, 2 * pair, 2, "l"), ACT.Copy)
+            lower[blk, pair] = ring.tile([P, 2, BLK], F32, name="lower", bufs=6)
+            nc.scalar.activation(lower[blk, pair][:], first_product(("lower",), blk, 2 * pair, 2, "l"), ACT.Copy)
 
         def combine(blk, jc0, count):
             b, half = divmod(blk, 2)
             pair, within = divmod(jc0, 2)
             low = lower[blk, pair][:, within : within + count, :]
             diff = ring.tile([P, count, BLK], F32, name="diff")
-            nc.vector.tensor_tensor(diff[:], first_product("upper", blk, jc0, count, "u"), low, ALU.subtract)
+            nc.vector.tensor_tensor(diff[:], first_product(("upper",), blk, jc0, count, "u"), low, ALU.subtract)
             dist = ring.tile([P, count, BLK], F32, name="dist", bufs=4)
             nc.scalar.activation(dist[:], diff[:], ACT.Abs)
             weighted = ring.tile([P, count, BLK], F32, name="weighted")
-            nc.vector.tensor_tensor(weighted[:], first_product("traffic", blk, jc0, count, "t"), dist[:], ALU.mult)
+            nc.vector.tensor_tensor(weighted[:], first_product(("traffic",), blk, jc0, count, "t"), dist[:], ALU.mult)
             adder = nc.gpsimd if (blk, pair) in add_on_gpsimd else nc.vector
             adder.tensor_tensor(
                 h[b, pair][:, within : within + count, half * BLK : (half + 1) * BLK], weighted[:], low, ALU.add
+            )
+
+        def keep_lower(pair):
+            lower[LAST, pair] = first_product(("lower",), LAST, 2 * pair, 2, "l")
+
+        def combine_last(jc0, count):
+            pair, within = divmod(jc0, 2)
+            dist = ring.tile([P, count, BLK], F32, name="dist", bufs=4)
+            nc.scalar.activation(dist[:], first_product(("lower", "upper"), LAST, jc0, count, "u"), ACT.Abs)
+            weighted = ring.tile([P, count, BLK], F32, name="weighted")
+            nc.vector.tensor_tensor(weighted[:], first_product(("traffic",), LAST, jc0, count, "t"), dist[:], ALU.mult)
+            nc.vector.tensor_tensor(
+                h[1, pair][:, within : within + count, BLK:],
+                lower[LAST, pair][:, within : within + count, :],
+                weighted[:],
+                ALU.add,
             )
 
         def make_h(b, jc0, count, tag):
@@ -245,7 +269,7 @@ def tile_list_rule_shadowing_conflicts_kernel(
             per_bank = 4 // count
             for g, tag in enumerate(tags):
                 bank = psum.tile([P, per_bank, width], F32, name="bank_y", tag=tag, bufs=banks[tag])
-                for n, b in enumerate((1, 0)):
+                for n, b in enumerate((0, 1)):
                     codes, plane, c0 = hq[b, jc0]
                     for i in range(per_bank):
                         nt = g * per_bank + i
@@ -264,43 +288,36 @@ def tile_list_rule_shadowing_conflicts_kernel(
                     nc.vector.scalar_tensor_tensor(
                         result[:, i, :], bank[:, i, :], gain_t[:, nt : nt + 1], res_t[:, nt, cols], ALU.mult, ALU.add
                     )
-                rows = out.rearrange("(t p) j -> p t j", p=P)[:, g * per_bank : (g + 1) * per_bank, cols]
-                nc.sync.dma_start(rows, result[:])
+                    nc.sync.dma_start(out[nt * P : (nt + 1) * P, cols], result[:, i, :])
 
-        for a in range(PASSES):
-            quantize_w("lower", a, 0)
-        for a in range(PASSES):
-            quantize_w("upper", a, 0)
-        for a in range(PASSES):
-            quantize_w("lower", a, 1)
-        for a in range(PASSES):
-            quantize_w("upper", a, 1)
+
+        quantize_w("lower", 0)
+        quantize_w("upper", 0)
         for pair in range(2):
             copy_lower(0, pair)
+        quantize_w("lower", 1)
+        quantize_w("upper", 1)
         for pair in range(2):
             copy_lower(1, pair)
-        for a in range(PASSES):
-            quantize_w("lower", a, 2)
-        for a in range(PASSES):
-            quantize_w("lower", a, 3)
         combine(0, 0, 2)
         combine(0, 2, 2)
-        combine(1, 0, 2)
-        combine(1, 2, 2)
+        quantize_w("lower", 2)
+        quantize_w("upper", 2)
         for pair in range(2):
             copy_lower(2, pair)
-        for pair in range(2):
-            copy_lower(3, pair)
-        for a in range(PASSES):
-            quantize_w("upper", a, 2)
-        for a in range(PASSES):
-            quantize_w("upper", a, 3)
-        make_h(0, 0, 2, "h")
-        make_h(0, 2, 2, "h")
+        combine(1, 0, 2)
+        combine(1, 2, 2)
+        quantize_w("lower", 3)
+        quantize_w("upper", 3)
         combine(2, 0, 2)
         combine(2, 2, 2)
-        for jc in range(4):
-            combine(3, jc, 1)
-        for jc in range(4):
-            make_h(1, jc, 1, "h")
-            finish(jc, 1, ("l",))
+        make_h(0, 0, 2, "h")
+        make_h(0, 2, 2, "h")
+        keep_lower(0)
+        keep_lower(1)
+        combine_last(0, 2)
+        combine_last(2, 2)
+        make_h(1, 0, 2, "h")
+        make_h(1, 2, 2, "h")
+        finish(0, 2, ("u", "u"))
+        finish(2, 2, ("t", "t"))

@@ -20,9 +20,20 @@ ACT = mybir.ActivationFunctionType
 P = 128
 PACK = 4
 K_PASS = P * PACK
-BLK = 256
 PASSES = 2
-LAST = 3
+QUADRANTS = 4
+PLANE_ROWS = 4
+BLK = 256
+BLOCKS = H // BLK
+LAST = BLOCKS - 1
+GROUPS = S // P
+PAIRS = (slice(0, 2), slice(2, 4))
+ROW_TILES = N // P
+
+PIECES = [(name, a, blk) for blk in range(BLOCKS) for name in ("lower", "upper") for a in range(PASSES)]
+FIRST_PIECES = 3
+PIECES_BEFORE_TABLE_1 = 6
+PIECES_BEFORE_W2 = 7
 
 
 def tile_list_rule_shadowing_conflicts_kernel(
@@ -31,293 +42,222 @@ def tile_list_rule_shadowing_conflicts_kernel(
     nc = tc.nc
     with ExitStack() as ctx:
         keep = ctx.enter_context(tc.tile_pool(name="keep", bufs=1))
-        ring = ctx.enter_context(tc.tile_pool(name="ring", bufs=3))
+        ring = ctx.enter_context(tc.tile_pool(name="ring", bufs=2))
         psum = ctx.enter_context(tc.psum_pool(name="psum", bufs=2))
-
-        lists = {}
-
-        def load_list(name):
-            lists[name] = keep.tile([P, S // 16], U16, name=f"list_{name}")
-            nc.sync.dma_start(lists[name][:], {"lower": offs3, "upper": offs, "traffic": offs2}[name])
 
         tab_sc = keep.tile([P, T], U8, align_bytes=64)
         w2_sc = keep.tile([P, PASSES, H], U8, align_bytes=64)
         w4_sc = keep.tile([P, N], U8, align_bytes=64)
         traffic_sc1 = keep.tile([P, S], U8, align_bytes=64)
-        nc.vector.memset(w2_sc[:].rearrange("p a c -> p (a c)").bitcast(I32), 0)
+        nc.gpsimd.memset(w2_sc[:].rearrange("p a c -> p (a c)").bitcast(I32), 0)
         nc.vector.memset(tab_sc[:].bitcast(I32), 0)
         nc.vector.memset(w4_sc[:].bitcast(I32), 0)
         nc.vector.memset(traffic_sc1[:].bitcast(I32), 0)
-
-        def load_tab_scales():
-            for q in range(4):
-                nc.sync.dma_start(
-                    tab_sc[32 * q : 32 * q + 8, :].bitcast(I32), tab_scales[:, 4 * q : 4 * q + 4, :].bitcast(I32)
-                )
-
-        def load_w2_scales(eng):
-            for q in range(4):
-                eng.dma_start(
-                    w2_sc[32 * q : 32 * q + 4, :, :].bitcast(I32),
-                    w2_scales[:, 4 * q : 4 * q + 4, :].rearrange("a r c -> r a c").bitcast(I32),
-                )
-
         ident = keep.tile([P, P], F32)
         make_identity(nc, ident[:])
 
-        tab = [keep.tile([P, T], I32, name=f"tab{a}", align_bytes=64) for a in range(PASSES)]
+        table = [keep.tile([P, T], I32, name=f"table{a}", align_bytes=64) for a in range(PASSES)]
         w2_t = keep.tile([P, PASSES, 2 * H], U8, align_bytes=64)
         w4_t = keep.tile([P, PASSES, N], I32, align_bytes=64)
-        res_t = keep.tile([P, 4, S], F32)
-        gain_t = keep.tile([P, 4], F32)
-        raw = {}
+        res_t = keep.tile([P, ROW_TILES, S], F32)
+        gain_t = keep.tile([P, ROW_TILES], F32)
+        lists, raw, words, scales = {}, {}, {}, {}
 
-        def load_tab(a, pieces):
-            src = tab_words[a].rearrange("p t i -> p (t i)").bitcast(I32)
-            for i in range(pieces):
-                cols = slice(i * T // pieces, (i + 1) * T // pieces)
-                nc.sync.dma_start(tab[a][:, cols], src[:, cols])
+        def load_list(name):
+            lists[name] = keep.tile([P, S // 16], U16, name=f"list_{name}")
+            nc.sync.dma_start(lists[name][:], {"lower": offs3, "upper": offs, "traffic": offs2}[name])
 
-        def load_gain():
-            with nc.allow_non_contiguous_dma(reason="one gain a partition"):
-                nc.sync.dma_start(gain_t[:], gain.rearrange("(t p) -> p t", p=P))
+        def table_words(a):
+            return tab_words[a].rearrange("p t i -> p (t i)").bitcast(I32)
 
-        def load_w4_scales(eng):
-            for q in range(4):
-                eng.dma_start(
-                    w4_sc[32 * q : 32 * q + 8, :].bitcast(I32), w4_scales[:, 4 * q : 4 * q + 4, :].bitcast(I32)
-                )
+        def load_packed_planes(tile, planes):
+            for q in range(QUADRANTS):
+                rows = planes[:, PLANE_ROWS * q : PLANE_ROWS * (q + 1), :]
+                nc.sync.dma_start(tile[32 * q : 32 * q + PASSES * PLANE_ROWS, :].bitcast(I32), rows.bitcast(I32))
 
-        def load_w(name, a, blk, nblk):
-            src = {"lower": w3, "upper": w1}[name]
-            t = keep.tile([P, PACK, nblk * BLK], F32, name=f"raw_{name}{a}_{blk}")
-            rows = src[a * K_PASS : (a + 1) * K_PASS, blk * BLK : (blk + nblk) * BLK]
-            nc.sync.dma_start(t[:], rows.rearrange("(p j) c -> p j c", j=PACK))
-            for i in range(nblk):
-                raw[name, a, blk + i] = t[:, :, i * BLK : (i + 1) * BLK]
-
-        def load_w4():
-            nc.sync.dma_start(w4_t[:], w4_words.rearrange("a p c i -> p a (c i)").bitcast(I32))
-
-        def load_res():
-            nc.sync.dma_start(res_t[:], res.rearrange("(t p) j -> p t j", p=P))
-
-        def load_w2():
-            nc.sync.dma_start(w2_t[:].bitcast(I32), w2_words.rearrange("a p c -> p a c").bitcast(I32))
-
-        load_list("lower")
-        load_list("upper")
-        load_list("traffic")
-        load_tab(0, 2)
-        load_tab_scales()
-        load_w2_scales(nc.gpsimd)
-        load_w4_scales(nc.gpsimd)
-        load_w("lower", 0, 0, 1)
-        load_w("lower", 1, 0, 1)
-        load_w("upper", 0, 0, 1)
-
-        words, scales = {}, {}
+        def load_piece(name, a, blk):
+            raw[name, a, blk] = keep.tile([P, PACK, BLK], F32, name=f"raw_{name}{a}_{blk}")
+            rows = {"lower": w3, "upper": w1}[name][a * K_PASS : (a + 1) * K_PASS, blk * BLK : (blk + 1) * BLK]
+            nc.sync.dma_start(raw[name, a, blk][:], rows.rearrange("(p j) c -> p j c", j=PACK))
 
         def gather_words(name, a):
             words[name, a] = keep.tile([P, S], U32, name=f"words_{name}{a}", align_bytes=64)
-            nc.vector.tensor_copy(words[name, a][:], tab[a][:].bitcast(U32).indirect(lists[name][:]))
+            nc.vector.tensor_copy(words[name, a][:], table[a][:].bitcast(U32).indirect(lists[name][:]))
 
         def gather_scales(name):
-            g = keep.tile([P, S], U8, name=f"scales_{name}", align_bytes=64)
-            nc.vector.tensor_copy(g[:], tab_sc[:].indirect(lists[name][:]))
-            scales[name, 0] = g[:]
-            scales[name, 1] = g[4:P, :]
+            gathered = keep.tile([P, S], U8, name=f"scales_{name}", align_bytes=64)
+            nc.vector.tensor_copy(gathered[:], tab_sc[:].indirect(lists[name][:]))
+            for a in range(PASSES):
+                scales[name, a] = gathered[PLANE_ROWS * a : P, :]
 
-        def shift_traffic_scales(eng):
-            eng.dma_start(traffic_sc1[0:100, :].bitcast(I32), scales["traffic", 0][4:104, :].bitcast(I32))
-            scales["traffic", 1] = traffic_sc1[:]
+        load_list("lower")
+        for half in (slice(0, T // 2), slice(T // 2, T)):
+            nc.sync.dma_start(table[0][:, half], table_words(0)[:, half])
+        load_list("upper")
+        load_list("traffic")
+        load_packed_planes(tab_sc, tab_scales)
+        for q in range(QUADRANTS):
+            rows = w2_scales[:, PLANE_ROWS * q : PLANE_ROWS * (q + 1), :].rearrange("a i c -> i a c")
+            nc.gpsimd.dma_start(w2_sc[32 * q : 32 * q + PLANE_ROWS, :, :].bitcast(I32), rows.bitcast(I32))
+        for piece in PIECES[:FIRST_PIECES]:
+            load_piece(*piece)
 
         for name in ("lower", "upper", "traffic"):
             gather_words(name, 0)
         gather_scales("traffic")
-        shift_traffic_scales(nc.sync)
-        load_w("upper", 1, 0, 1)
-        load_w("lower", 0, 1, 1)
-        load_w("lower", 1, 1, 1)
-        load_tab(1, 1)
-        load_w("upper", 0, 1, 1)
-        load_w2()
-        load_w("upper", 1, 1, 1)
-        load_w("lower", 0, 2, 1)
-        load_w("lower", 1, 2, 1)
-        load_w("upper", 0, 2, 1)
-        load_w("upper", 1, 2, 1)
-        load_w("lower", 0, 3, 1)
-        load_w("lower", 1, 3, 1)
-        load_w("upper", 0, 3, 1)
-        load_w("upper", 1, 3, 1)
-        load_gain()
-        load_w4()
-        load_res()
+        last_row = 32 * (QUADRANTS - 1) + PLANE_ROWS
+        nc.sync.dma_start(traffic_sc1[:last_row, :].bitcast(I32), scales["traffic", 1][:last_row, :].bitcast(I32))
+        scales["traffic", 1] = traffic_sc1[:]
+
+        for piece in PIECES[FIRST_PIECES:PIECES_BEFORE_TABLE_1]:
+            load_piece(*piece)
+        nc.sync.dma_start(table[1][:], table_words(1))
+        for piece in PIECES[PIECES_BEFORE_TABLE_1:PIECES_BEFORE_W2]:
+            load_piece(*piece)
+        nc.sync.dma_start(w2_t[:].bitcast(I32), w2_words.rearrange("a p c -> p a c").bitcast(I32))
+        for piece in PIECES[PIECES_BEFORE_W2:]:
+            load_piece(*piece)
+        nc.sync.dma_start(w4_t[:], w4_words.rearrange("a p c i -> p a (c i)").bitcast(I32))
+        load_packed_planes(w4_sc, w4_scales)
+        nc.sync.dma_start(res_t[:], res.rearrange("(t p) j -> p t j", p=P))
+        with nc.allow_non_contiguous_dma(reason="gain[128 t + p] is one value of partition p"):
+            nc.sync.dma_start(gain_t[:], gain.rearrange("(t p) -> p t", p=P))
+
         gather_scales("lower")
         gather_scales("upper")
         for name in ("lower", "upper", "traffic"):
             gather_words(name, 1)
 
-        wq, wq_sc = {}, {}
-        banks = {"l": 2, "u": 2, "t": 2, "h": 2}
-        on_vector = {("upper", 1, 1), ("upper", 1, 2), ("upper", 1, 3)}
-        on_gpsimd = set()
+        wq, wq_sc, lower, hq = {}, {}, {}, {}
+        h = [keep.tile([P, GROUPS, K_PASS], BF16, name=f"h{a}") for a in range(PASSES)]
 
-        def quantize_w(name, blk):
+        def quantize_block(name, blk):
             grouped = ring.tile([P, PASSES, BLK, PACK], BF16, name="grouped", align_bytes=64, bufs=5)
-            sign = -1.0 if (name, blk) == ("upper", LAST) else 1.0
+            negate = (name, blk) == ("upper", LAST)
             for a in range(PASSES):
                 dst = grouped[:, a, :, :].rearrange("p (c i) t -> p c t i", i=4)
-                src = raw[name, a, blk].rearrange("p t (c i) -> p c t i", i=4)
-                if (name, a, blk) in on_vector and sign == 1.0:
-                    nc.vector.tensor_copy(dst, src)
-                elif (name, a, blk) in on_vector:
-                    nc.vector.tensor_scalar(dst, src, sign, None, ALU.mult)
+                src = raw[name, a, blk][:].rearrange("p t (c i) -> p c t i", i=4)
+                on_vector = name == "upper" and a == PASSES - 1 and blk >= 1
+                if not on_vector:
+                    nc.scalar.activation(dst, src, ACT.Copy, scale=-1.0 if negate else 1.0)
+                elif negate:
+                    nc.vector.tensor_scalar(dst, src, -1.0, None, ALU.mult)
                 else:
-                    nc.scalar.activation(dst, src, ACT.Copy, scale=sign)
+                    nc.vector.tensor_copy(dst, src)
             codes = keep.tile([P, PASSES * BLK], U32, name=f"wq_{name}{blk}", align_bytes=64)
-            plane = keep.tile([P, PASSES * BLK], U8, name=f"wqsc_{name}{blk}", align_bytes=64)
+            plane = keep.tile([P, PASSES * BLK], U8, name=f"wq_sc_{name}{blk}", align_bytes=64)
             nc.vector.quantize_mx(codes[:].bitcast(FP8X4), plane[:], grouped[:].rearrange("p a c t -> p (a c t)"))
             for a in range(PASSES):
-                wq[name, a, blk] = codes[:, a * BLK : (a + 1) * BLK]
+                wq[name, a, blk] = codes[:, a * BLK : (a + 1) * BLK].bitcast(FP8X4)
                 wq_sc[name, a, blk] = plane[:, a * BLK : (a + 1) * BLK]
 
-        def first_product(names, blk, jc0, count, tag):
-            bank = psum.tile([P, count, BLK], F32, name=f"bank_{names[-1]}", tag=tag, bufs=banks[tag])
-            steps = [(name, a, i) for name in names for i in range(count) for a in range(PASSES)]
-            for n, (name, a, i) in enumerate(steps):
-                cols = slice((jc0 + i) * P, (jc0 + i + 1) * P)
+        def first_product(names, blk, pair, tag):
+            bank = psum.tile([P, 2, BLK], F32, name=f"bank_{names[-1]}", tag=tag)
+            steps = [(name, i, a) for name in names for i in range(2) for a in range(PASSES)]
+            for n, (name, i, a) in enumerate(steps):
+                entries = slice((pair.start + i) * P, (pair.start + i + 1) * P)
                 if name == "traffic":
-                    rhs = w2_t[:, a, 2 * blk * BLK : 2 * (blk + 1) * BLK].bitcast(FP4X4)
-                    rhs_sc = w2_sc[:, a, blk * BLK : (blk + 1) * BLK]
+                    weights = w2_t[:, a, 2 * blk * BLK : 2 * (blk + 1) * BLK].bitcast(FP4X4)
+                    weights_sc = w2_sc[:, a, blk * BLK : (blk + 1) * BLK]
                 else:
-                    rhs = wq[name, a, blk].bitcast(FP8X4)
-                    rhs_sc = wq_sc[name, a, blk]
+                    weights, weights_sc = wq[name, a, blk], wq_sc[name, a, blk]
                 nc.tensor.matmul_mx(
                     bank[:, i, :],
-                    lhsT=words[name, a][:, cols].bitcast(FP8X4),
-                    lhsT_scale=scales[name, a][:, cols],
-                    rhs=rhs,
-                    rhs_scale=rhs_sc,
+                    lhsT=words[name, a][:, entries].bitcast(FP8X4),
+                    lhsT_scale=scales[name, a][:, entries],
+                    rhs=weights,
+                    rhs_scale=weights_sc,
                     start=(n == 0),
                     stop=(n == len(steps) - 1),
                 )
             return bank[:]
 
-        lower, h, hq, hq_sc = {}, {}, {}, {}
-        add_on_gpsimd = set()
-        for b in range(PASSES):
-            for pair in range(2):
-                h[b, pair] = keep.tile([P, 2, K_PASS], BF16, name=f"h{b}{pair}")
+        def copy_lower(blk):
+            lower[blk] = ring.tile([P, GROUPS, BLK], F32, name="lower", bufs=LAST)
+            for pair in PAIRS:
+                nc.scalar.activation(lower[blk][:, pair, :], first_product(("lower",), blk, pair, "l"), ACT.Copy)
 
-        def copy_lower(blk, pair):
-            lower[blk, pair] = ring.tile([P, 2, BLK], F32, name="lower", bufs=6)
-            nc.scalar.activation(lower[blk, pair][:], first_product(("lower",), blk, 2 * pair, 2, "l"), ACT.Copy)
+        def weigh(dist, blk):
+            weighted = ring.tile([P, GROUPS, BLK], F32, name="weighted")
+            for pair in PAIRS:
+                traffic = first_product(("traffic",), blk, pair, "t")
+                nc.vector.tensor_tensor(weighted[:, pair, :], traffic, dist[:, pair, :], ALU.mult)
+            return weighted
 
-        def combine(blk, jc0, count):
-            b, half = divmod(blk, 2)
-            pair, within = divmod(jc0, 2)
-            low = lower[blk, pair][:, within : within + count, :]
-            diff = ring.tile([P, count, BLK], F32, name="diff")
-            nc.vector.tensor_tensor(diff[:], first_product(("upper",), blk, jc0, count, "u"), low, ALU.subtract)
-            dist = ring.tile([P, count, BLK], F32, name="dist", bufs=4)
-            nc.scalar.activation(dist[:], diff[:], ACT.Abs)
-            weighted = ring.tile([P, count, BLK], F32, name="weighted")
-            nc.vector.tensor_tensor(weighted[:], first_product(("traffic",), blk, jc0, count, "t"), dist[:], ALU.mult)
-            adder = nc.gpsimd if (blk, pair) in add_on_gpsimd else nc.vector
-            adder.tensor_tensor(
-                h[b, pair][:, within : within + count, half * BLK : (half + 1) * BLK], weighted[:], low, ALU.add
-            )
+        def h_block(blk, pair):
+            a, half = divmod(blk, K_PASS // BLK)
+            return h[a][:, pair, half * BLK : (half + 1) * BLK]
 
-        def keep_lower(pair):
-            lower[LAST, pair] = first_product(("lower",), LAST, 2 * pair, 2, "l")
+        def combine(blk):
+            diff = ring.tile([P, GROUPS, BLK], F32, name="diff")
+            dist = ring.tile([P, GROUPS, BLK], F32, name="dist")
+            for pair in PAIRS:
+                upper = first_product(("upper",), blk, pair, "u")
+                nc.vector.tensor_tensor(diff[:, pair, :], upper, lower[blk][:, pair, :], ALU.subtract)
+            for pair in PAIRS:
+                nc.scalar.activation(dist[:, pair, :], diff[:, pair, :], ACT.Abs)
+            weighted = weigh(dist, blk)
+            for pair in PAIRS:
+                nc.vector.tensor_tensor(h_block(blk, pair), weighted[:, pair, :], lower[blk][:, pair, :], ALU.add)
 
-        def combine_last(jc0, count):
-            pair, within = divmod(jc0, 2)
-            dist = ring.tile([P, count, BLK], F32, name="dist", bufs=4)
-            nc.scalar.activation(dist[:], first_product(("lower", "upper"), LAST, jc0, count, "u"), ACT.Abs)
-            weighted = ring.tile([P, count, BLK], F32, name="weighted")
-            nc.vector.tensor_tensor(weighted[:], first_product(("traffic",), LAST, jc0, count, "t"), dist[:], ALU.mult)
-            nc.vector.tensor_tensor(
-                h[1, pair][:, within : within + count, BLK:],
-                lower[LAST, pair][:, within : within + count, :],
-                weighted[:],
-                ALU.add,
-            )
+        def combine_last():
+            dist = ring.tile([P, GROUPS, BLK], F32, name="dist")
+            lower_banks = [first_product(("lower",), LAST, pair, "l") for pair in PAIRS]
+            for pair in PAIRS:
+                nc.scalar.activation(dist[:, pair, :], first_product(("lower", "upper"), LAST, pair, "u"), ACT.Abs)
+            weighted = weigh(dist, LAST)
+            for pair, bank in zip(PAIRS, lower_banks):
+                nc.vector.tensor_tensor(h_block(LAST, pair), bank, weighted[:, pair, :], ALU.add)
 
-        def make_h(b, jc0, count, tag):
-            bank = psum.tile([P, count, 2, P], F32, name="bank_h", tag=tag, bufs=banks[tag])
-            for i in range(count):
-                pair, within = divmod(jc0 + i, 2)
-                pairs = h[b, pair][:, within, :].bitcast(F32)
+        def quantize_h(a, pair):
+            bank = psum.tile([P, 2, 2, P], F32, name="bank_h", tag="h")
+            for i in range(2):
+                h_words = h[a][:, pair.start + i, :].bitcast(F32)
                 for u in range(2):
-                    nc.tensor.transpose(bank[:, i, u, :], pairs[:, u::2], ident[:])
-            h_t = ring.tile([P, count, P, 2], F32, name="h_t", align_bytes=64)
-            nc.scalar.copy(h_t[:], bank[:].rearrange("p i u j -> p i j u"))
-            codes = keep.tile([P, count * P], U32, name=f"hq{b}{jc0}", align_bytes=64)
-            plane = keep.tile([P, count * P], U8, name=f"hqsc{b}{jc0}", align_bytes=64)
-            nc.vector.quantize_mx(
-                codes[:].bitcast(FP8X4), plane[:], h_t[:].rearrange("p i j u -> p (i j u)").bitcast(BF16)
-            )
-            for i in range(count):
-                hq[b, jc0 + i] = (codes, plane, i * P)
+                    nc.tensor.transpose(bank[:, i, u, :], h_words[:, u::2], ident[:])
+            turned = ring.tile([P, 2, P, 2], F32, name="turned", align_bytes=64)
+            nc.scalar.copy(turned[:], bank[:].rearrange("p i u j -> p i j u"))
+            codes = keep.tile([P, 2 * P], U32, name=f"hq{a}{pair.start}", align_bytes=64)
+            plane = keep.tile([P, 2 * P], U8, name=f"hq_sc{a}{pair.start}", align_bytes=64)
+            values = turned[:].rearrange("p i j u -> p (i j u)").bitcast(BF16)
+            nc.vector.quantize_mx(codes[:].bitcast(FP8X4), plane[:], values)
+            hq[a, pair.start] = (codes[:].bitcast(FP8X4), plane[:])
 
-        def finish(jc0, count, tags):
-            width = count * P
-            cols = slice(jc0 * P, jc0 * P + width)
-            per_bank = 4 // count
-            for g, tag in enumerate(tags):
-                bank = psum.tile([P, per_bank, width], F32, name="bank_y", tag=tag, bufs=banks[tag])
-                for n, b in enumerate((0, 1)):
-                    codes, plane, c0 = hq[b, jc0]
-                    for i in range(per_bank):
-                        nt = g * per_bank + i
+        def finish(pair, tag):
+            entries = slice(pair.start * P, pair.stop * P)
+            for first in range(0, ROW_TILES, 2):
+                bank = psum.tile([P, 2, 2 * P], F32, name="bank_y", tag=tag)
+                for a in range(PASSES):
+                    codes, plane = hq[a, pair.start]
+                    for i in range(2):
+                        rows = slice((first + i) * P, (first + i + 1) * P)
                         nc.tensor.matmul_mx(
                             bank[:, i, :],
-                            lhsT=w4_t[:, b, nt * P : (nt + 1) * P].bitcast(FP8X4),
-                            lhsT_scale=w4_sc[4 * b : P, nt * P : (nt + 1) * P],
-                            rhs=codes[:, c0 : c0 + width].bitcast(FP8X4),
-                            rhs_scale=plane[:, c0 : c0 + width],
-                            start=(n == 0 and i == 0),
-                            stop=(n == 1 and i == per_bank - 1),
+                            lhsT=w4_t[:, a, rows].bitcast(FP8X4),
+                            lhsT_scale=w4_sc[PLANE_ROWS * a : P, rows],
+                            rhs=codes,
+                            rhs_scale=plane,
+                            start=(a == 0 and i == 0),
+                            stop=(a == PASSES - 1 and i == 1),
                         )
-                result = keep.tile([P, per_bank, width], F32, name=f"result{jc0}{g}")
-                for i in range(per_bank):
-                    nt = g * per_bank + i
+                result = keep.tile([P, 2, 2 * P], F32, name=f"result{pair.start}{first}")
+                for i in range(2):
+                    t = first + i
                     nc.vector.scalar_tensor_tensor(
-                        result[:, i, :], bank[:, i, :], gain_t[:, nt : nt + 1], res_t[:, nt, cols], ALU.mult, ALU.add
+                        result[:, i, :], bank[:, i, :], gain_t[:, t : t + 1], res_t[:, t, entries], ALU.mult, ALU.add
                     )
-                    nc.sync.dma_start(out[nt * P : (nt + 1) * P, cols], result[:, i, :])
+                    nc.sync.dma_start(out[t * P : (t + 1) * P, entries], result[:, i, :])
 
-
-        quantize_w("lower", 0)
-        quantize_w("upper", 0)
-        for pair in range(2):
-            copy_lower(0, pair)
-        quantize_w("lower", 1)
-        quantize_w("upper", 1)
-        for pair in range(2):
-            copy_lower(1, pair)
-        combine(0, 0, 2)
-        combine(0, 2, 2)
-        quantize_w("lower", 2)
-        quantize_w("upper", 2)
-        for pair in range(2):
-            copy_lower(2, pair)
-        combine(1, 0, 2)
-        combine(1, 2, 2)
-        quantize_w("lower", 3)
-        quantize_w("upper", 3)
-        combine(2, 0, 2)
-        combine(2, 2, 2)
-        make_h(0, 0, 2, "h")
-        make_h(0, 2, 2, "h")
-        keep_lower(0)
-        keep_lower(1)
-        combine_last(0, 2)
-        combine_last(2, 2)
-        make_h(1, 0, 2, "h")
-        make_h(1, 2, 2, "h")
-        finish(0, 2, ("u", "u"))
-        finish(2, 2, ("t", "t"))
+        for blk in range(BLOCKS):
+            quantize_block("lower", blk)
+            quantize_block("upper", blk)
+            if blk < LAST:
+                copy_lower(blk)
+            if blk >= 1:
+                combine(blk - 1)
+        combine_last()
+        for a in range(PASSES):
+            for pair in PAIRS:
+                quantize_h(a, pair)
+        for pair, tag in zip(PAIRS, ("u", "t")):
+            finish(pair, tag)

@@ -135,9 +135,10 @@ def tile_list_rule_shadowing_conflicts_kernel(
             grouped = ring.tile([P, PASSES, BLK, PACK], BF16, name="grouped", align_bytes=64, bufs=5)
             negate = (name, blk) == ("upper", LAST)
             for a in range(PASSES):
-                dst = grouped[:, a, :, :].rearrange("p (c i) t -> p c t i", i=4)
-                src = raw[name, a, blk][:].rearrange("p t (c i) -> p c t i", i=4)
                 on_vector = name == "upper" and a == PASSES - 1 and blk >= 1
+                run = 4 if on_vector else 2
+                dst = grouped[:, a, :, :].rearrange("p (c i) t -> p c t i", i=run)
+                src = raw[name, a, blk][:].rearrange("p t (c i) -> p c t i", i=run)
                 if not on_vector:
                     nc.scalar.activation(dst, src, ACT.Copy, scale=-1.0 if negate else 1.0)
                 elif negate:

from contextlib import ExitStack

import concourse.mybir as mybir
from concourse.masks import make_identity

K, H, N, T, S = 1024, 1024, 512, 2048, 512
FLOPS = 2 * (3 * K * H * S + H * N * S)

F32 = mybir.dt.float32
BF16 = mybir.dt.bfloat16
I32 = mybir.dt.int32
U32 = mybir.dt.uint32
U16 = mybir.dt.uint16
U8 = mybir.dt.uint8
FP8X4 = mybir.dt.float8_e4m3fn_x4
FP4X4 = mybir.dt.float4_e2m1fn_x4
ALU = mybir.AluOpType
ACT = mybir.ActivationFunctionType

P = 128
PACK = 4
K_PASS = P * PACK
PASSES = 2
QUADRANTS = 4
PLANE_ROWS = 4
BLK = 256
BLOCKS = H // BLK
LAST = BLOCKS - 1
GROUPS = S // P
PAIRS = (slice(0, 2), slice(2, 4))
ROW_TILES = N // P

PIECES = [(name, a, blk) for blk in range(BLOCKS) for name in ("lower", "upper") for a in range(PASSES)]
FIRST_PIECES = 3
PIECES_BEFORE_TABLE_1 = 6
PIECES_BEFORE_W2 = 7


def tile_list_rule_shadowing_conflicts_kernel(
    tc, tab_words, tab_scales, offs, offs2, offs3, w1, w2_words, w2_scales, w3, w4_words, w4_scales, gain, res, out
):
    nc = tc.nc
    with ExitStack() as ctx:
        keep = ctx.enter_context(tc.tile_pool(name="keep", bufs=1))
        ring = ctx.enter_context(tc.tile_pool(name="ring", bufs=2))
        psum = ctx.enter_context(tc.psum_pool(name="psum", bufs=2))

        tab_sc = keep.tile([P, T], U8, align_bytes=64)
        w2_sc = keep.tile([P, PASSES, H], U8, align_bytes=64)
        w4_sc = keep.tile([P, N], U8, align_bytes=64)
        traffic_sc1 = keep.tile([P, S], U8, align_bytes=64)
        nc.gpsimd.memset(w2_sc[:].rearrange("p a c -> p (a c)").bitcast(I32), 0)
        nc.vector.memset(tab_sc[:].bitcast(I32), 0)
        nc.vector.memset(w4_sc[:].bitcast(I32), 0)
        nc.vector.memset(traffic_sc1[:].bitcast(I32), 0)
        ident = keep.tile([P, P], F32)
        make_identity(nc, ident[:])

        table = [keep.tile([P, T], I32, name=f"table{a}", align_bytes=64) for a in range(PASSES)]
        w2_t = keep.tile([P, PASSES, 2 * H], U8, align_bytes=64)
        w4_t = keep.tile([P, PASSES, N], I32, align_bytes=64)
        res_t = keep.tile([P, ROW_TILES, S], F32)
        gain_t = keep.tile([P, ROW_TILES], F32)
        lists, raw, words, scales = {}, {}, {}, {}

        def load_list(name):
            lists[name] = keep.tile([P, S // 16], U16, name=f"list_{name}")
            nc.sync.dma_start(lists[name][:], {"lower": offs3, "upper": offs, "traffic": offs2}[name])

        def table_words(a):
            return tab_words[a].rearrange("p t i -> p (t i)").bitcast(I32)

        def load_packed_planes(tile, planes):
            for q in range(QUADRANTS):
                rows = planes[:, PLANE_ROWS * q : PLANE_ROWS * (q + 1), :]
                nc.sync.dma_start(tile[32 * q : 32 * q + PASSES * PLANE_ROWS, :].bitcast(I32), rows.bitcast(I32))

        def load_piece(name, a, blk):
            raw[name, a, blk] = keep.tile([P, PACK, BLK], F32, name=f"raw_{name}{a}_{blk}")
            rows = {"lower": w3, "upper": w1}[name][a * K_PASS : (a + 1) * K_PASS, blk * BLK : (blk + 1) * BLK]
            nc.sync.dma_start(raw[name, a, blk][:], rows.rearrange("(p j) c -> p j c", j=PACK))

        def gather_words(name, a):
            words[name, a] = keep.tile([P, S], U32, name=f"words_{name}{a}", align_bytes=64)
            nc.vector.tensor_copy(words[name, a][:], table[a][:].bitcast(U32).indirect(lists[name][:]))

        def gather_scales(name):
            gathered = keep.tile([P, S], U8, name=f"scales_{name}", align_bytes=64)
            nc.vector.tensor_copy(gathered[:], tab_sc[:].indirect(lists[name][:]))
            for a in range(PASSES):
                scales[name, a] = gathered[PLANE_ROWS * a : P, :]

        load_list("lower")
        for half in (slice(0, T // 2), slice(T // 2, T)):
            nc.sync.dma_start(table[0][:, half], table_words(0)[:, half])
        load_list("upper")
        load_list("traffic")
        load_packed_planes(tab_sc, tab_scales)
        for q in range(QUADRANTS):
            rows = w2_scales[:, PLANE_ROWS * q : PLANE_ROWS * (q + 1), :].rearrange("a i c -> i a c")
            nc.gpsimd.dma_start(w2_sc[32 * q : 32 * q + PLANE_ROWS, :, :].bitcast(I32), rows.bitcast(I32))
        for piece in PIECES[:FIRST_PIECES]:
            load_piece(*piece)

        for name in ("lower", "upper", "traffic"):
            gather_words(name, 0)
        gather_scales("traffic")
        last_row = 32 * (QUADRANTS - 1) + PLANE_ROWS
        nc.sync.dma_start(traffic_sc1[:last_row, :].bitcast(I32), scales["traffic", 1][:last_row, :].bitcast(I32))
        scales["traffic", 1] = traffic_sc1[:]

        for piece in PIECES[FIRST_PIECES:PIECES_BEFORE_TABLE_1]:
            load_piece(*piece)
        nc.sync.dma_start(table[1][:], table_words(1))
        for piece in PIECES[PIECES_BEFORE_TABLE_1:PIECES_BEFORE_W2]:
            load_piece(*piece)
        nc.sync.dma_start(w2_t[:].bitcast(I32), w2_words.rearrange("a p c -> p a c").bitcast(I32))
        for piece in PIECES[PIECES_BEFORE_W2:]:
            load_piece(*piece)
        nc.sync.dma_start(w4_t[:], w4_words.rearrange("a p c i -> p a (c i)").bitcast(I32))
        load_packed_planes(w4_sc, w4_scales)
        nc.sync.dma_start(res_t[:], res.rearrange("(t p) j -> p t j", p=P))
        with nc.allow_non_contiguous_dma(reason="gain[128 t + p] is one value of partition p"):
            nc.sync.dma_start(gain_t[:], gain.rearrange("(t p) -> p t", p=P))

        gather_scales("lower")
        gather_scales("upper")
        for name in ("lower", "upper", "traffic"):
            gather_words(name, 1)

        wq, wq_sc, lower, hq = {}, {}, {}, {}
        h = [keep.tile([P, GROUPS, K_PASS], BF16, name=f"h{a}") for a in range(PASSES)]

        def quantize_block(name, blk):
            grouped = ring.tile([P, PASSES, BLK, PACK], BF16, name="grouped", align_bytes=64, bufs=5)
            negate = (name, blk) == ("upper", LAST)
            for a in range(PASSES):
                on_vector = name == "upper" and a == PASSES - 1 and blk >= 1
                run = 4 if on_vector else 2
                dst = grouped[:, a, :, :].rearrange("p (c i) t -> p c t i", i=run)
                src = raw[name, a, blk][:].rearrange("p t (c i) -> p c t i", i=run)
                if not on_vector:
                    nc.scalar.activation(dst, src, ACT.Copy, scale=-1.0 if negate else 1.0)
                elif negate:
                    nc.vector.tensor_scalar(dst, src, -1.0, None, ALU.mult)
                else:
                    nc.vector.tensor_copy(dst, src)
            codes = keep.tile([P, PASSES * BLK], U32, name=f"wq_{name}{blk}", align_bytes=64)
            plane = keep.tile([P, PASSES * BLK], U8, name=f"wq_sc_{name}{blk}", align_bytes=64)
            nc.vector.quantize_mx(codes[:].bitcast(FP8X4), plane[:], grouped[:].rearrange("p a c t -> p (a c t)"))
            for a in range(PASSES):
                wq[name, a, blk] = codes[:, a * BLK : (a + 1) * BLK].bitcast(FP8X4)
                wq_sc[name, a, blk] = plane[:, a * BLK : (a + 1) * BLK]

        def first_product(names, blk, pair, tag):
            bank = psum.tile([P, 2, BLK], F32, name=f"bank_{names[-1]}", tag=tag)
            steps = [(name, i, a) for name in names for i in range(2) for a in range(PASSES)]
            for n, (name, i, a) in enumerate(steps):
                entries = slice((pair.start + i) * P, (pair.start + i + 1) * P)
                if name == "traffic":
                    weights = w2_t[:, a, 2 * blk * BLK : 2 * (blk + 1) * BLK].bitcast(FP4X4)
                    weights_sc = w2_sc[:, a, blk * BLK : (blk + 1) * BLK]
                else:
                    weights, weights_sc = wq[name, a, blk], wq_sc[name, a, blk]
                nc.tensor.matmul_mx(
                    bank[:, i, :],
                    lhsT=words[name, a][:, entries].bitcast(FP8X4),
                    lhsT_scale=scales[name, a][:, entries],
                    rhs=weights,
                    rhs_scale=weights_sc,
                    start=(n == 0),
                    stop=(n == len(steps) - 1),
                )
            return bank[:]

        def copy_lower(blk):
            lower[blk] = ring.tile([P, GROUPS, BLK], F32, name="lower", bufs=LAST)
            for pair in PAIRS:
                nc.scalar.activation(lower[blk][:, pair, :], first_product(("lower",), blk, pair, "l"), ACT.Copy)

        def weigh(dist, blk):
            weighted = ring.tile([P, GROUPS, BLK], F32, name="weighted")
            for pair in PAIRS:
                traffic = first_product(("traffic",), blk, pair, "t")
                nc.vector.tensor_tensor(weighted[:, pair, :], traffic, dist[:, pair, :], ALU.mult)
            return weighted

        def h_block(blk, pair):
            a, half = divmod(blk, K_PASS // BLK)
            return h[a][:, pair, half * BLK : (half + 1) * BLK]

        def combine(blk):
            diff = ring.tile([P, GROUPS, BLK], F32, name="diff")
            dist = ring.tile([P, GROUPS, BLK], F32, name="dist")
            for pair in PAIRS:
                upper = first_product(("upper",), blk, pair, "u")
                nc.vector.tensor_tensor(diff[:, pair, :], upper, lower[blk][:, pair, :], ALU.subtract)
            for pair in PAIRS:
                nc.scalar.activation(dist[:, pair, :], diff[:, pair, :], ACT.Abs)
            weighted = weigh(dist, blk)
            for pair in PAIRS:
                nc.vector.tensor_tensor(h_block(blk, pair), weighted[:, pair, :], lower[blk][:, pair, :], ALU.add)

        def combine_last():
            dist = ring.tile([P, GROUPS, BLK], F32, name="dist")
            lower_banks = [first_product(("lower",), LAST, pair, "l") for pair in PAIRS]
            for pair in PAIRS:
                nc.scalar.activation(dist[:, pair, :], first_product(("lower", "upper"), LAST, pair, "u"), ACT.Abs)
            weighted = weigh(dist, LAST)
            for pair, bank in zip(PAIRS, lower_banks):
                nc.vector.tensor_tensor(h_block(LAST, pair), bank, weighted[:, pair, :], ALU.add)

        def quantize_h(a, pair):
            bank = psum.tile([P, 2, 2, P], F32, name="bank_h", tag="h")
            for i in range(2):
                h_words = h[a][:, pair.start + i, :].bitcast(F32)
                for u in range(2):
                    nc.tensor.transpose(bank[:, i, u, :], h_words[:, u::2], ident[:])
            turned = ring.tile([P, 2, P, 2], F32, name="turned", align_bytes=64)
            nc.scalar.copy(turned[:], bank[:].rearrange("p i u j -> p i j u"))
            codes = keep.tile([P, 2 * P], U32, name=f"hq{a}{pair.start}", align_bytes=64)
            plane = keep.tile([P, 2 * P], U8, name=f"hq_sc{a}{pair.start}", align_bytes=64)
            values = turned[:].rearrange("p i j u -> p (i j u)").bitcast(BF16)
            nc.vector.quantize_mx(codes[:].bitcast(FP8X4), plane[:], values)
            hq[a, pair.start] = (codes[:].bitcast(FP8X4), plane[:])

        def finish(pair, tag):
            entries = slice(pair.start * P, pair.stop * P)
            for first in range(0, ROW_TILES, 2):
                bank = psum.tile([P, 2, 2 * P], F32, name="bank_y", tag=tag)
                for a in range(PASSES):
                    codes, plane = hq[a, pair.start]
                    for i in range(2):
                        rows = slice((first + i) * P, (first + i + 1) * P)
                        nc.tensor.matmul_mx(
                            bank[:, i, :],
                            lhsT=w4_t[:, a, rows].bitcast(FP8X4),
                            lhsT_scale=w4_sc[PLANE_ROWS * a : P, rows],
                            rhs=codes,
                            rhs_scale=plane,
                            start=(a == 0 and i == 0),
                            stop=(a == PASSES - 1 and i == 1),
                        )
                result = keep.tile([P, 2, 2 * P], F32, name=f"result{pair.start}{first}")
                for i in range(2):
                    t = first + i
                    nc.vector.scalar_tensor_tensor(
                        result[:, i, :], bank[:, i, :], gain_t[:, t : t + 1], res_t[:, t, entries], ALU.mult, ALU.add
                    )
                    nc.sync.dma_start(out[t * P : (t + 1) * P, entries], result[:, i, :])

        for blk in range(BLOCKS):
            quantize_block("lower", blk)
            quantize_block("upper", blk)
            if blk < LAST:
                copy_lower(blk)
            if blk >= 1:
                combine(blk - 1)
        combine_last()
        for a in range(PASSES):
            for pair in PAIRS:
                quantize_h(a, pair)
        for pair, tag in zip(PAIRS, ("u", "t")):
            finish(pair, tag)
